import numpy as np, ml_dtypes
CORES = [6,14,22,30,38,46,54,62,70,78,86,94,102,110,118,126,196,197,198,199]
N = 20
T = 64
ROUTE = [[[0,2],[12,15],[12,8],[15,16],[5,13],[10,1],[11,17],[13,7],[6,15],[6,17],[10,11],[19,8],[0,1],[0,17],[3,0],[9,15],[5,4],[1,11],[14,10],[19,18],[2,6],[16,9],[0,12],[7,3],[6,14],[8,17],[2,19],[4,5],[0,5],[0,10],[12,4],[6,16],[17,5],[4,8],[12,6],[12,11],[3,9],[1,8],[10,0],[6,17],[13,16],[3,0],[8,2],[5,12],[6,7],[8,1],[17,4],[11,3],[14,17],[16,11],[3,9],[11,12],[14,15],[11,5],[11,4],[5,15],[4,10],[11,6],[4,2],[6,5],[19,11],[13,16],[8,0],[8,4]],[[17,18],[7,12],[5,17],[11,18],[17,10],[16,0],[7,19],[13,6],[17,2],[8,13],[12,18],[4,9],[0,9],[12,0],[19,12],[5,7],[13,17],[6,7],[14,16],[6,3],[18,1],[18,0],[8,15],[1,18],[17,19],[3,0],[18,11],[2,1],[10,11],[16,18],[6,2],[1,5],[9,3],[13,15],[19,1],[17,3],[6,11],[5,15],[12,7],[4,2],[9,4],[1,12],[16,17],[9,6],[10,19],[6,14],[1,12],[15,17],[7,1],[10,3],[12,2],[17,10],[17,1],[15,3],[3,5],[2,1],[0,7],[16,13],[10,6],[3,17],[0,1],[12,2],[0,3],[0,18]],[[19,7],[17,14],[9,11],[5,4],[7,12],[1,3],[14,2],[16,2],[10,3],[11,7],[3,0],[9,11],[14,11],[6,18],[5,18],[12,13],[8,0],[15,1],[13,9],[15,9],[7,13],[15,17],[1,9],[10,0],[5,16],[0,1],[6,3],[12,3],[2,14],[17,3],[8,14],[10,3],[17,2],[13,5],[8,19],[7,14],[2,5],[2,3],[14,11],[1,3],[6,1],[5,14],[13,7],[8,5],[2,14],[3,19],[14,5],[14,17],[9,14],[5,18],[4,19],[17,5],[17,8],[0,13],[8,16],[15,8],[11,9],[19,2],[17,19],[15,0],[5,15],[14,12],[19,8],[8,13]],[[9,14],[5,19],[2,17],[8,13],[14,18],[0,19],[17,18],[11,4],[12,19],[0,18],[4,8],[19,7],[1,9],[11,19],[13,8],[16,1],[15,0],[15,13],[1,13],[14,8],[17,14],[0,12],[19,11],[5,12],[9,7],[2,10],[3,11],[17,1],[10,0],[3,17],[7,16],[8,6],[19,15],[3,19],[16,17],[5,11],[6,17],[3,12],[18,11],[3,4],[0,7],[8,9],[16,1],[3,7],[10,19],[9,14],[19,7],[5,2],[4,14],[2,6],[4,2],[14,18],[4,9],[14,9],[0,19],[17,14],[9,16],[2,4],[10,13],[10,8],[18,19],[18,13],[17,0],[2,15]],[[1,10],[1,19],[7,18],[18,16],[18,7],[8,11],[9,4],[9,2],[8,2],[14,2],[3,15],[16,8],[1,10],[3,13],[4,12],[16,6],[11,7],[15,10],[11,6],[13,9],[2,18],[0,7],[4,14],[15,6],[7,0],[9,8],[4,5],[11,1],[8,12],[11,19],[5,0],[17,8],[13,2],[5,15],[17,8],[2,18],[18,16],[6,10],[13,3],[6,1],[3,18],[2,7],[18,1],[9,11],[16,10],[8,10],[16,13],[7,16],[15,12],[4,17],[5,7],[9,15],[4,12],[18,15],[12,17],[15,5],[5,12],[9,12],[13,0],[3,0],[2,4],[10,1],[5,17],[4,12]],[[3,18],[11,4],[6,2],[2,7],[3,17],[19,10],[6,5],[18,0],[14,2],[8,10],[16,12],[1,9],[1,16],[2,5],[12,2],[9,14],[17,6],[2,10],[13,16],[10,16],[18,3],[18,16],[12,17],[16,5],[16,12],[12,7],[19,14],[10,13],[19,15],[10,11],[17,16],[14,17],[3,13],[14,13],[9,11],[16,3],[4,18],[4,11],[7,4],[0,16],[17,4],[17,18],[4,5],[17,16],[7,1],[17,14],[16,13],[8,11],[12,14],[14,12],[14,6],[8,7],[16,1],[7,1],[7,4],[13,12],[17,18],[0,17],[19,8],[0,7],[13,18],[5,9],[0,8],[13,8]],[[14,10],[4,13],[15,5],[17,19],[4,12],[4,6],[8,19],[8,12],[3,4],[14,12],[8,7],[0,7],[14,18],[18,4],[13,9],[9,7],[17,0],[15,4],[12,19],[9,12],[1,17],[16,6],[10,14],[13,17],[17,0],[3,16],[11,15],[8,19],[8,2],[4,13],[3,14],[6,2],[4,16],[2,12],[16,3],[18,8],[7,18],[8,2],[2,13],[14,2],[13,6],[12,17],[1,5],[9,3],[4,0],[8,0],[14,5],[11,16],[2,16],[8,2],[0,5],[5,4],[7,0],[12,15],[13,9],[6,18],[19,3],[7,8],[4,10],[3,14],[13,17],[12,1],[9,16],[2,4]],[[0,5],[10,17],[9,11],[11,0],[19,10],[19,9],[1,12],[11,5],[17,10],[12,14],[14,18],[9,10],[17,14],[4,13],[10,6],[15,2],[11,12],[7,15],[14,1],[12,14],[16,18],[11,5],[9,6],[9,0],[17,16],[8,13],[8,14],[5,6],[10,2],[9,13],[3,6],[4,11],[11,1],[10,13],[19,15],[18,2],[15,1],[4,14],[0,18],[6,19],[9,12],[13,10],[9,1],[19,13],[14,10],[19,15],[4,8],[9,14],[2,16],[15,11],[12,11],[0,16],[6,1],[9,13],[12,4],[8,4],[9,10],[8,16],[7,16],[4,12],[16,8],[9,12],[0,14],[7,0]],[[6,12],[11,9],[0,18],[8,10],[6,2],[19,3],[11,17],[17,9],[16,2],[3,15],[3,15],[8,17],[18,0],[2,15],[3,17],[19,18],[6,13],[6,4],[10,19],[10,13],[0,1],[11,18],[13,10],[4,6],[17,1],[10,2],[0,16],[13,0],[9,8],[3,4],[6,17],[14,9],[8,13],[19,7],[13,11],[2,14],[10,11],[8,2],[1,15],[14,17],[3,19],[4,3],[16,10],[12,1],[17,8],[2,7],[12,2],[5,16],[10,8],[1,17],[15,7],[4,2],[19,1],[17,11],[2,12],[16,8],[14,11],[9,19],[19,6],[6,0],[3,14],[10,1],[16,6],[2,16]],[[16,8],[12,2],[0,8],[9,5],[18,1],[19,10],[3,0],[14,13],[11,1],[4,13],[9,15],[14,4],[12,2],[0,7],[10,16],[4,14],[9,7],[19,4],[17,16],[18,16],[3,17],[18,1],[14,3],[7,17],[13,7],[6,3],[18,14],[10,18],[0,4],[8,14],[11,12],[11,1],[13,5],[3,17],[5,15],[15,7],[2,3],[16,18],[5,0],[2,1],[16,5],[17,4],[19,16],[1,18],[18,9],[6,15],[16,17],[15,14],[19,18],[4,0],[0,6],[10,2],[15,8],[15,9],[11,9],[17,7],[3,1],[16,3],[5,19],[7,17],[18,16],[6,3],[8,14],[1,12]],[[15,9],[0,15],[1,12],[6,15],[7,17],[2,14],[11,0],[4,19],[4,14],[9,0],[8,19],[5,0],[13,5],[14,10],[8,19],[0,10],[3,13],[5,14],[5,4],[9,0],[9,8],[15,2],[6,17],[16,1],[10,2],[6,8],[7,10],[0,12],[16,1],[6,11],[16,0],[10,3],[12,10],[18,14],[3,14],[5,19],[12,1],[3,4],[13,8],[17,5],[15,13],[3,6],[16,7],[4,9],[18,13],[16,11],[4,13],[12,3],[1,0],[3,5],[10,19],[14,18],[15,8],[8,5],[18,10],[19,17],[2,15],[11,9],[15,10],[11,5],[10,4],[6,11],[3,8],[11,19]],[[4,5],[18,2],[10,3],[9,17],[15,4],[2,12],[0,10],[11,0],[18,5],[13,7],[15,3],[16,18],[10,2],[15,2],[5,10],[6,10],[7,12],[19,6],[12,4],[6,17],[4,18],[18,7],[4,18],[6,16],[11,5],[3,7],[3,19],[3,5],[1,8],[12,13],[7,19],[0,15],[9,18],[11,16],[7,11],[15,10],[19,14],[3,17],[11,9],[12,10],[18,16],[14,3],[4,9],[5,0],[11,15],[1,14],[10,5],[15,5],[19,2],[5,19],[15,0],[10,9],[7,12],[14,13],[15,17],[18,13],[9,1],[3,9],[10,13],[13,19],[16,7],[2,0],[16,11],[10,0]],[[16,6],[12,18],[2,6],[16,0],[15,3],[14,1],[16,11],[9,1],[16,12],[18,6],[12,10],[0,10],[19,14],[5,3],[6,10],[9,19],[2,8],[14,19],[11,0],[11,3],[2,17],[15,11],[1,19],[8,10],[17,10],[15,1],[15,4],[19,2],[10,14],[3,10],[3,13],[13,0],[4,19],[9,15],[5,17],[8,19],[10,16],[8,11],[12,15],[1,6],[18,6],[10,3],[3,4],[18,5],[7,8],[19,2],[10,11],[12,0],[10,18],[11,3],[17,6],[19,5],[19,5],[17,15],[11,14],[14,5],[3,13],[15,9],[6,17],[16,19],[6,8],[18,9],[1,0],[17,4]],[[1,16],[17,5],[4,11],[3,0],[0,15],[13,5],[18,11],[0,3],[1,11],[11,0],[19,15],[19,6],[17,4],[18,9],[13,10],[18,12],[3,16],[9,11],[1,8],[4,6],[19,6],[16,4],[19,5],[2,7],[2,15],[13,16],[8,1],[2,16],[9,1],[4,8],[5,19],[17,1],[0,5],[4,0],[13,19],[19,14],[17,15],[14,12],[0,11],[19,2],[19,2],[13,0],[3,10],[13,0],[16,0],[2,0],[7,5],[19,7],[16,10],[1,2],[5,8],[16,2],[6,2],[7,2],[2,17],[13,10],[9,2],[3,19],[0,1],[1,15],[11,10],[9,19],[8,7],[6,19]],[[6,13],[2,10],[17,12],[6,10],[3,18],[4,11],[1,17],[14,4],[18,8],[1,8],[0,5],[12,13],[1,10],[14,13],[9,4],[10,5],[0,9],[2,13],[18,12],[10,17],[18,7],[7,1],[5,1],[5,7],[15,16],[4,6],[1,6],[13,4],[0,13],[3,14],[8,11],[6,7],[4,17],[11,13],[12,15],[8,6],[8,19],[18,17],[12,11],[17,16],[7,3],[12,17],[5,13],[1,10],[15,18],[17,13],[13,10],[14,17],[7,2],[2,10],[1,19],[11,12],[18,19],[8,19],[3,0],[3,15],[18,15],[10,11],[12,10],[8,1],[2,0],[2,8],[0,5],[12,9]],[[16,19],[15,10],[7,16],[11,8],[13,8],[4,1],[17,14],[0,8],[15,16],[10,8],[4,19],[11,0],[16,10],[7,19],[2,11],[10,3],[17,13],[17,18],[7,12],[16,7],[16,4],[12,2],[4,18],[16,8],[6,19],[14,12],[6,18],[13,19],[5,7],[16,15],[5,9],[10,2],[15,4],[9,4],[9,0],[14,3],[9,18],[15,10],[12,2],[15,5],[1,11],[13,2],[11,0],[13,8],[1,7],[13,2],[12,19],[19,7],[13,3],[15,4],[6,19],[19,10],[2,16],[17,3],[1,2],[3,15],[18,19],[3,17],[2,16],[9,14],[3,4],[13,1],[11,19],[17,11]],[[14,9],[18,19],[15,19],[10,18],[14,18],[9,11],[0,18],[19,14],[10,9],[7,18],[7,4],[2,3],[7,4],[3,13],[7,16],[7,12],[12,11],[1,14],[16,9],[3,9],[8,3],[12,16],[3,9],[2,18],[6,17],[13,18],[4,11],[0,10],[4,3],[0,15],[18,19],[12,14],[6,13],[2,16],[18,19],[13,18],[17,15],[6,11],[6,14],[1,8],[19,8],[3,8],[4,9],[7,19],[4,19],[0,16],[8,7],[5,4],[16,18],[1,10],[2,7],[14,13],[16,6],[16,12],[8,14],[10,16],[15,18],[8,7],[2,9],[17,3],[10,6],[15,9],[3,19],[11,13]],[[8,18],[3,6],[18,17],[15,7],[9,0],[3,2],[15,12],[9,14],[12,0],[9,14],[3,4],[10,16],[13,10],[3,2],[15,18],[13,11],[2,8],[5,2],[13,8],[18,13],[4,14],[17,9],[12,15],[19,6],[16,0],[12,11],[8,10],[2,15],[19,3],[5,0],[8,1],[9,7],[12,6],[18,14],[7,0],[9,10],[13,6],[11,6],[4,19],[18,1],[7,2],[19,4],[16,0],[4,16],[15,8],[4,0],[1,13],[14,4],[11,16],[2,16],[11,15],[16,9],[10,9],[14,8],[19,4],[16,10],[5,6],[13,18],[8,13],[2,7],[0,19],[16,15],[16,15],[4,17]],[[9,17],[8,0],[14,15],[12,3],[9,3],[1,9],[17,16],[14,16],[11,7],[11,16],[18,17],[11,2],[18,12],[11,14],[6,17],[16,1],[2,14],[8,6],[17,7],[1,2],[0,14],[16,0],[12,7],[9,0],[19,15],[6,16],[10,6],[18,17],[7,10],[17,7],[1,5],[1,12],[13,10],[5,2],[17,6],[3,12],[19,2],[14,5],[16,19],[8,16],[12,7],[7,14],[1,2],[8,12],[11,0],[4,10],[13,8],[13,16],[8,10],[14,9],[17,11],[6,11],[14,11],[15,11],[19,14],[16,15],[8,14],[14,19],[0,15],[8,0],[1,15],[19,15],[6,15],[1,0]],[[0,19],[19,15],[13,11],[13,1],[9,15],[11,1],[18,1],[14,11],[9,18],[3,9],[18,6],[17,15],[16,15],[15,1],[0,13],[14,8],[8,17],[8,19],[4,9],[14,1],[0,10],[3,11],[7,3],[13,7],[1,17],[19,6],[3,5],[1,10],[11,4],[8,19],[4,0],[11,17],[10,18],[2,19],[18,13],[14,3],[2,10],[5,18],[19,13],[7,9],[13,6],[2,16],[3,8],[11,0],[5,3],[1,4],[8,3],[1,2],[7,17],[9,3],[12,5],[15,11],[19,11],[14,18],[15,16],[12,4],[16,9],[17,6],[1,5],[16,6],[18,16],[0,19],[12,7],[0,13]]]
YW = 142
def setup_inputs(rng):
    return {"x": rng.standard_normal((N, 128, T), dtype=np.float32).astype(ml_dtypes.bfloat16)}
def reference(x):
    y = np.full((N, 128, YW), np.nan, x.dtype)
    fill = [0] * N
    for r in range(N):
        for t in range(T):
            for e in ROUTE[r][t]:
                y[e][:, fill[e]] = x[r][:, t]
                fill[e] += 1
    return {"y": y}

from concourse.bass import DstId, RemoteDMATransfer

NW_ALONE = 4
NW_SHARED = 4
HCAP = 10
RCAP = 12

SCRATCH = {
    "xs": ("sbuf", [128, 64], "bfloat16"),
    "land": ("sbuf", [128, 142], "bfloat16"),
}
for _k in sorted({NW_ALONE, NW_SHARED}):
    SCRATCH["xd%d" % _k] = ("dram", [_k, 128, 64 // _k], "bfloat16")
SEMAPHORES = ["loc", "fed", "arr"]

_CACHE = {}


def _bits(m):
    return [i for i in range(m.bit_length()) if (m >> i) & 1]


def _widths(m, ne):
    p = 1
    while p < m:
        p *= 2
    w = [ne // p] * m
    spare = ne - sum(w)
    for i in range(m):
        if spare >= w[i]:
            spare -= w[i]
            w[i] *= 2
    return w


def _pack(items, engines):
    ne = len(engines)
    rounds = []
    if not items:
        return rounds
    for i in range(0, len(items), ne):
        part = items[i:i + ne]
        ws = _widths(len(part), ne)
        at = 0
        rnd = []
        for it, w in zip(part, ws):
            mask = 0
            for b in engines[at:at + w]:
                mask |= 1 << b
            at += w
            rnd.append((it, mask, w))
        rounds.append(rnd)
    return rounds


def _plan(T, topo):
    cores = list(T.cores)
    n = len(cores)
    route = T.tables["ROUTE"]
    nt = T.tables["T"]
    world = range((max(topo.host(c) for c in cores) + 1) * topo.CORES_PER_HOST)

    def where(c):
        return (topo.host(c), topo.chip(c))

    chips = {}
    for r in range(n):
        chips.setdefault(where(cores[r]), []).append(r)
    nw = [NW_ALONE if len(chips[where(cores[r])]) == 1 else NW_SHARED for r in range(n)]
    wd = [nt // k for k in nw]

    fill = [0] * n
    copies = [[] for _ in range(n)]
    for r in range(n):
        for t in range(nt):
            for e in route[r][t]:
                copies[r].append((t, e, fill[e]))
                fill[e] += 1

    can = {w: [w != cores[e] and topo.may_write(w, cores[e]) for e in range(n)] for w in world}
    near = {w: [where(w) == where(cores[e]) for e in range(n)] for w in world}
    feedable = {w: [w != c and topo.may_write(c, w) for c in cores] for w in world}

    def solve(r, helpers, hcap, rcap):
        rc = cores[r]
        cap = {}
        mem = {}
        opts = []
        for (t, e, col) in copies[r]:
            hs = helpers[t // wd[r]]
            o = [(w, 1) for w in hs if can[w][e] and near[w][e]]
            o += [(w, 0) for w in hs if can[w][e]]
            if can[rc][e]:
                if near[rc][e]:
                    o.append((rc, 1))
                o.append((rc, 0))
            opts.append(o)
            for k in o:
                if k not in cap:
                    cap[k] = rcap if k[0] == rc else hcap
                    mem[k] = []

        def aug(i, seen):
            for k in opts[i]:
                if k in seen:
                    continue
                seen.add(k)
                if len(mem[k]) < cap[k]:
                    mem[k].append(i)
                    return True
                for idx, j in enumerate(mem[k]):
                    if aug(j, seen):
                        mem[k][idx] = i
                        return True
            return False

        val = 0
        for i in range(len(opts)):
            if aug(i, set()):
                val += 1
        return val, mem

    helpers = [[[] for _ in range(nw[r])] for r in range(n)]

    def give(r, cands):
        groups = {}
        for w in cands:
            if feedable[w][r]:
                groups.setdefault((tuple(can[w]), tuple(near[w]), tuple(feedable[w])), []).append(w)
        best = None
        for k, ws in groups.items():
            for s in range(nw[r]):
                helpers[r][s].append(ws[0])
                v = solve(r, helpers[r], HCAP, RCAP)[0]
                helpers[r][s].pop()
                sc = (-v, sum(k[0]), sum(k[2]), len(helpers[r][s]), s)
                if best is None or sc < best[0]:
                    best = (sc, ws[0], s)
        if best is None:
            return False
        helpers[r][best[2]].append(best[1])
        cands.remove(best[1])
        return True

    idle = [w for w in world if w not in cores]
    for ch, rs in chips.items():
        loc = [w for w in idle if where(w) == ch]
        i = 0
        while loc and give(rs[i % len(rs)], loc):
            i += 1
    pool = [w for w in idle if where(w) not in chips]
    order = sorted(range(n), key=lambda r: sum(feedable[w][r] for w in pool))
    for r in order:
        while solve(r, helpers[r], HCAP, RCAP)[0] < len(copies[r]):
            if not give(r, pool):
                break

    prog = {}
    arrive = [0] * n

    def banks(w, dsts):
        lo = 0
        hi = 0
        first = True
        for d in dsts:
            m = topo.mask(w, d)
            lo = m if first else (lo & m)
            hi |= m
            first = False
        return _bits(lo), _bits(hi & ~lo)

    for r in range(n):
        rc = cores[r]
        hcap = 1
        while True:
            val, mem = solve(r, helpers[r], hcap, max(RCAP, hcap))
            if val == len(copies[r]):
                break
            hcap += 1
        work = {}
        for (w, bank), idxs in mem.items():
            work.setdefault(w, {0: [], 1: []})[bank] = sorted(idxs)
        slot_of = {w: s for s in range(nw[r]) for w in helpers[r][s]}
        for w in [rc] + sorted(slot_of):
            mine = work.get(w, {0: [], 1: []})
            lo, hi = banks(w, [c for c in cores if c != w and topo.may_write(w, c)])
            calls = []
            for bank, eng in ((0, lo), (1, hi)):
                for k, rnd in enumerate(_pack(mine[bank], eng)):
                    while len(calls) <= k:
                        calls.append([])
                    for i, mask, width in rnd:
                        t, e, col = copies[r][i]
                        calls[k].append((t, mask, width, cores[e], col))
                        arrive[e] += width
            prog[w] = {"rank": None, "slot": slot_of.get(w), "nw": nw[r], "fed": 0, "calls": calls, "feed": []}
        lo, hi = banks(rc, sorted(slot_of))
        far = [(s, [w for w in helpers[r][s] if where(w) != where(rc)]) for s in range(nw[r])]
        home = [(s, [w for w in helpers[r][s] if where(w) == where(rc)]) for s in range(nw[r])]
        if not hi:
            far = [(s, list(helpers[r][s])) for s in range(nw[r])]
            home = []
        feed = []
        for grp, eng in ((far, lo), (home, hi)):
            grp = [x for x in grp if x[1]]
            for rnd in _pack(grp, eng):
                for (s, ws), mask, width in rnd:
                    feed.append((s, mask, width, ws))
                    for w in ws:
                        prog[w]["fed"] += width
        prog[rc]["rank"] = r
        prog[rc]["feed"] = feed
    for r in range(n):
        prog[cores[r]]["arrive"] = arrive[r]
        prog[cores[r]]["count"] = fill[r]
    return prog


def rank_program(g, core, T, topo):
    if "plan" not in _CACHE:
        _CACHE["plan"] = _plan(T, topo)
    p = _CACHE["plan"].get(core)
    if p is None:
        return
    loc, fed, arr = T.sem.loc, T.sem.fed, T.sem.arr
    nw = p["nw"]
    wd = T.tables["T"] // nw
    xd = T["xd%d" % nw]

    def dst(d):
        rid, pid = topo.addr(d, core)
        return DstId(rid=rid, pnc=pid)

    nloc = 0
    if p["rank"] is not None:
        for s in range(nw):
            q = g.sync if s % 2 == 0 else g.scalar
            q.dma_start(xd[s], T.x[:, s * wd:(s + 1) * wd]).then_inc(loc, 16)
            nloc += 16
        g.scalar.dma_start(T.xs[:], T.x[:]).then_inc(fed, 16)
        g.wait_ge(loc, nloc)
        if p["feed"]:
            g.remote_dma_fused(
                [RemoteDMATransfer(dst_ids=[dst(w) for w in ws], dma_engine_mask=mask, remote_sem=fed,
                                   srcs=[xd[s]], dsts=[xd[s] for w in ws])
                 for (s, mask, width, ws) in p["feed"]], local_sem=loc)
            nloc += sum(f[2] for f in p["feed"])
        g.wait_ge(fed, 16)
    else:
        s = p["slot"]
        g.sync.wait_ge(fed, p["fed"])
        g.sync.dma_start(T.xs[:, s * wd:(s + 1) * wd], xd[s]).then_inc(loc, 16)
        nloc += 16
        g.wait_ge(fed, p["fed"])
        g.wait_ge(loc, nloc)
    for call in p["calls"]:
        g.remote_dma_fused(
            [RemoteDMATransfer(dst_ids=[dst(d)], dma_engine_mask=mask, remote_sem=arr,
                               srcs=[T.xs[:, t:t + 1]], dsts=[T.land[:, col:col + 1]])
             for (t, mask, width, d, col) in call], local_sem=loc)
        nloc += sum(c[2] for c in call)
    if p["rank"] is not None:
        cnt = p["count"]
        g.sync.wait_ge(arr, p["arrive"])
        g.sync.dma_start(T.y[:, 0:cnt], T.land[:, 0:cnt]).then_inc(loc, 16)
        nloc += 16
        g.wait_ge(arr, p["arrive"])
    g.wait_ge(loc, nloc)
